import numpy as np, ml_dtypes
CORES = [89,94,345,350]
N = 4
R, T, B = 8192, 4096, 256
def entries(a): return a.T.reshape(-1)
def pack(v, P): return np.ascontiguousarray(np.asarray(v, np.int32).reshape(-1, P).T)
def lists(rng, how):
    I = rng.integers(0, N * R, (N, T)); E = np.sort(rng.integers(0, T + 1, (N, B)), axis=1)
    if how == "void":
        E = np.zeros((N, B), np.int64)
        for r in range(N): k = np.sort(1 + rng.permutation(B - 2)[:6]); c = np.sort(1 + rng.permutation(T)[:6]); E[r] = np.concatenate([[0], c])[np.searchsorted(k, np.arange(B), side="right")]
        E[rng.integers(N)] = 0
    if how == "one":
        p = rng.permutation(N); z = rng.integers(0, B, N); z[p[0]] = 0; z[p[1]] = B - 1; E = np.where(np.arange(B)[None, :] < z[:, None], 0, T)
        I[p[::2]] = R * p[1] + I[p[::2]] % R
    if how == "single": E = np.broadcast_to(1 + np.arange(B), (N, B)).copy()
    if how == "hotrank": I = R * int(rng.integers(N)) + rng.integers(0, R, (N, T))
    if how == "edge": I = R * rng.integers(0, N, (N, T)) + np.where(rng.random((N, T)) < 0.5, 0, R - 1); E[:, -1] = T
    return {"idx": np.stack([pack(i, 16) for i in I]), "end": np.stack([pack(v, 16) for v in E])}
def setup_inputs(rng):
    return dict({"tab": rng.standard_normal((N, 128, R), dtype=np.float32).astype(ml_dtypes.bfloat16)}, **lists(rng, "uniform"))
def setup_inputs_edge(rng):
    d = setup_inputs(rng); d.update(lists(rng, "edge"))
    for k in ("tab",): d[k] = (d[k].astype(np.float32) * 1048576.0).astype(d[k].dtype)
    return d
def setup_inputs_hotrank(rng):
    d = setup_inputs(rng); d.update(lists(rng, "hotrank"))
    for k in ("tab",): d[k] = (d[k].astype(np.float32) * (1 / 1024.0)).astype(d[k].dtype)
    return d
def setup_inputs_one(rng):
    d = setup_inputs(rng); d.update(lists(rng, "one"))
    return d
def setup_inputs_single(rng):
    d = setup_inputs(rng); d.update(lists(rng, "single"))
    return d
def setup_inputs_void(rng):
    d = setup_inputs(rng); d.update(lists(rng, "void"))
    return d
def check_inputs(x):
    bad = []
    if x["idx"].min() < 0 or x["idx"].max() >= N * R: bad.append("idx out of range")
    if x["end"].min() < 0 or x["end"].max() >= T + 1: bad.append("end out of range")
    if any((np.diff(entries(a)) < 0).any() for a in x["end"]): bad.append("end falls")
    t = x["tab"].astype(np.float32)
    if t.min() < -1e30 or t.max() > 1e30: bad.append("tab beyond -1e30 to 1e30")
    return bad
def reference(tab, idx, end):
    A = np.concatenate(list(tab), axis=1)
    y = np.zeros((N, 128, B), tab.dtype)
    for r in range(N):
        G = A[:, entries(idx[r])]; c = np.concatenate([[0], entries(end[r])])
        for b in range(B):
            if c[b + 1] > c[b]: y[r][:, b] = G[:, c[b]:c[b + 1]].max(axis=1)
    return {"y": y}

@@ -1,0 +1,343 @@
+import numpy as np
+from concourse.mybir import dt, AluOpType, ActivationFunctionType
+
+R, NL, NB = 8192, 4096, 256
+PAD = 8
+W = 3 * PAD + 2 * R
+PW = R + 2 * PAD
+BIG = float(201 * 2.0 ** 92)
+ZC = NL + 7
+DUMP = NL + 8
+CAPW = DUMP + NB
+H = 1536
+HC, WC = H // 16, (NL - H) // 16
+HB = NB // 2
+FB = 1024
+
+
+def cuts(a, b):
+    n = (b - a) // 32
+    return [a, a + 32 * (n // 2), a + 32 * (n * 4 // 5), b]
+
+
+VH, VF, VO = 320, H + 704, 1152
+SH, SF, SO = cuts(VH, H), cuts(VF, NL), cuts(VO, NL)
+LOADS = [(0, 128, 0, 4096), (0, 64, 4096, 8192), (64, 128, 4096, 8192)]
+SWAPS = [(0, 4096, 2), (4096, 8192, 3)]
+
+SCRATCH = {
+    "win": ("sbuf", [128, W], "bfloat16"),
+    "ix": ("sbuf", [128, 256], "int32"),
+    "en": ("sbuf", [16, 16], "int32"),
+    "ep": ("sbuf", [16, 20], "int32"),
+    "dmp": ("sbuf", [16, 16], "float32"),
+    "pm": ("sbuf", [16, 128], "float32"),
+    "sel": ("sbuf", [16, 128], "float32"),
+    "eq": ("sbuf", [16, 16], "float32"),
+    "t1": ("sbuf", [16, 16], "float32"),
+    "q2": ("sbuf", [16, 16], "float32"),
+    "x1": ("sbuf", [16, 16], "float32"),
+    "u1": ("sbuf", [16, 16], "float32"),
+    "u2": ("sbuf", [16, 16], "float32"),
+    "pk": ("sbuf", [16, 48], "float32"),
+    "ta": ("sbuf", [128, 256], "int32"),
+    "tz": ("sbuf", [128, 256], "int32"),
+    "tc": ("sbuf", [128, 256], "int32"),
+    "td": ("sbuf", [128, 256], "int32"),
+    "lo": ("sbuf", [128, 2 * HC], "uint16"),
+    "ml": ("sbuf", [128, 2 * HC], "uint16"),
+    "fl": ("sbuf", [128, HC], "uint16"),
+    "fd": ("sbuf", [128, HC], "uint16"),
+    "eo": ("sbuf", [128, WC + 48], "uint16"),
+    "me": ("sbuf", [128, WC + 48], "uint16"),
+    "fe": ("sbuf", [128, WC + 32], "uint16"),
+    "de": ("sbuf", [128, 32], "uint16"),
+    "he": ("sbuf", [128, 16], "uint16"),
+    "oo": ("sbuf", [128, 256], "uint16"),
+    "neg": ("sbuf", [128, 256], "bfloat16"),
+    "cap": ("sbuf", [128, CAPW], "bfloat16"),
+    "capo": ("sbuf", [128, NL], "bfloat16"),
+    "capf": ("sbuf", [128, CAPW], "bfloat16"),
+    "capd": ("sbuf", [128, CAPW], "bfloat16"),
+    "go": ("sbuf", [128, NL], "bfloat16"),
+    "gf": ("sbuf", [128, NL], "bfloat16"),
+    "gd": ("sbuf", [128, H], "bfloat16"),
+    "so": ("sbuf", [128, NL + 8], "bfloat16"),
+    "sf": ("sbuf", [128, NL + 8], "bfloat16"),
+    "sd": ("sbuf", [128, H + 8], "bfloat16"),
+    "pd": ("sbuf", [128, NB], "bfloat16"),
+    "pm2": ("sbuf", [128, NB], "bfloat16"),
+    "pf": ("sbuf", [128, NB], "bfloat16"),
+    "pr": ("sbuf", [128, NB], "bfloat16"),
+    "ph": ("sbuf", [128, NB], "bfloat16"),
+    "yo": ("sbuf", [128, NB], "bfloat16"),
+    "ps": ("psum", [128, 48], "float32"),
+}
+NV, NS = 80, 20
+SEMAPHORES = (["ldi", "lde", "sty", "lst", "lsd", "ends", "end2", "hend", "ocap", "mate", "half", "prt0", "prt1",
+               "fin", "sent", "io_d", "io_p", "pe"]
+              + ["tb%d" % k for k in range(len(LOADS))] + ["sc%d" % k for k in range(NS)] + ["v%d" % k for k in range(NV)])
+
+_plan = {}
+
+
+def make_plan(T, topo):
+    if _plan:
+        return _plan
+    cores = list(T.cores)
+    n = len(cores)
+    allc = range(512)
+    chip = lambda c, x: topo.host(c) == topo.host(x) and topo.chip(c) == topo.chip(x)
+    here = lambda c, x: chip(c, x) and topo.die(c) == topo.die(x)
+    for i in range(n):
+        r = cores[i]
+        mate = [j for j in range(n) if j != i and chip(cores[j], r)][0]
+        far = [j for j in range(n) if topo.host(cores[j]) != topo.host(r) and topo.die(cores[j]) == topo.die(r)][0]
+        f = cores[far]
+        fm = [c for c in cores if c != f and chip(c, f)][0]
+        place = [c for c in allc if here(c, r)].index(r)
+        rel = [c for c in allc if topo.host(c) not in (topo.host(r), topo.host(f))
+               and topo.rack(topo.host(c)) == topo.rack(topo.host(r)) and topo.chip(c) == topo.chip(r) and topo.die(c) == topo.die(r)
+               and topo.may_write(r, c) and topo.may_write(c, f) and topo.may_write(c, fm) and topo.may_write(f, c) and topo.may_write(c, r)]
+        helper = [c for c in allc if here(c, r) and c not in cores][0]
+        _plan[i] = {"mate": mate, "far": far, "relay": rel[place], "helper": helper}
+    return _plan
+
+
+def bits(m):
+    return bin(m).count("1")
+
+
+def push(g, T, topo, core, dst, out, src, sem):
+    rid, pid = topo.addr(dst, core)
+    m = topo.mask(core, dst)
+    g.remote_dma(out, src, T.sem[sem], T.sem.sent, pid, rid, m)
+    return bits(m)
+
+
+def relay_program(g, core, T, topo, r, f, fm):
+    n = bits(topo.mask(r, core))
+    g.wait_ge(T.sem.lst, n)
+    k = push(g, T, topo, core, f, T.fl[:], T.ml[:, 0:HC], "lst")
+    k += push(g, T, topo, core, fm, T.fd[:], T.ml[:, HC:2 * HC], "lsd")
+    g.wait_ge(T.sem.ends, n)
+    k += push(g, T, topo, core, fm, T.de[:], T.me[:, WC + 16:WC + 48], "end2")
+    k += push(g, T, topo, core, f, T.fe[:], T.me[:, 0:WC + 32], "ends")
+    g.wait_ge(T.sem.prt0, bits(topo.mask(f, core)))
+    k += push(g, T, topo, core, r, T.ph[:, 0:HB], T.pr[:, 0:HB], "fin")
+    g.wait_ge(T.sem.prt1, n)
+    k += push(g, T, topo, core, f, T.ph[:, HB:NB], T.pr[:, HB:NB], "fin")
+    g.wait_ge(T.sem.sent, k)
+
+
+def helper_program(g, core, T, topo, r):
+    V = g.vector
+    V.memset(T.neg[:, :], -BIG).then_inc(T.sem.v0, 1)
+    V.memset(T.cap[:, :], BIG).then_inc(T.sem.v1, 1)
+    V.wait_ge(T.sem.v0, 1)
+    V.wait_ge(T.sem.v1, 1)
+    V.wait_ge(T.sem.hend, bits(topo.mask(r, core)))
+    V.tensor_copy(T.cap[:, :].indirect(T.he[:, :]), T.neg[:, :]).then_inc(T.sem.v2, 1)
+    g.wait_ge(T.sem.v2, 1)
+    k = push(g, T, topo, core, r, T.capo[:], T.cap[:, 0:NL], "ocap")
+    g.wait_ge(T.sem.sent, k)
+
+
+def rank_program(g, core, T, topo):
+    plan = make_plan(T, topo)
+    cores = list(T.cores)
+    rank = T.rank_of(core)
+    if rank is None:
+        for i in plan:
+            far = plan[i]["far"]
+            if plan[i]["relay"] == core:
+                relay_program(g, core, T, topo, cores[i], cores[far], cores[plan[far]["mate"]])
+            if plan[i]["helper"] == core:
+                helper_program(g, core, T, topo, cores[i])
+        return
+    mate, far, helper = plan[rank]["mate"], plan[rank]["far"], plan[rank]["helper"]
+    fmate = plan[far]["mate"]
+    mcore = cores[mate]
+    out_relay, in_relay, other_relay = plan[rank]["relay"], plan[far]["relay"], plan[fmate]["relay"]
+    base = R * min(rank, mate)
+    fbase = R * min(far, fmate)
+    low = (rank * R - base) // R * (R + PAD)
+    mine = low + PAD
+    V, S, Y = g.vector, g.scalar, g.sync
+    sem = T.sem
+    A = AluOpType
+    COPY = ActivationFunctionType.Copy
+    nv, ns = [0], [0]
+
+    def vs():
+        nv[0] += 1
+        return sem["v%d" % (nv[0] - 1)]
+
+    def ss():
+        ns[0] += 1
+        return sem["sc%d" % (ns[0] - 1)]
+
+    for k in range(4):
+        Y.dma_start(T.ix[16 * k:16 * k + 16, :], T.idx[:, :]).then_inc(sem.ldi, 16)
+    for k in range(4, 8):
+        S.dma_start(T.ix[16 * k:16 * k + 16, :], T.idx[:, :]).then_inc(sem.ldi, 16)
+    Y.dma_start(T.en[:, :], T.end[:, :]).then_inc(sem.lde, 16)
+    S.dma_start(T.ep[1:16, 3:19], T.end[0:15, :]).then_inc(sem.lde, 16)
+    S.dma_start(T.ep[0:1, 4:19], T.end[15:16, 0:15]).then_inc(sem.lde, 16)
+
+    def load(c):
+        p, q, a, b = LOADS[c]
+        Y.dma_start(T.win[p:q, mine + a:mine + b], T.tab[p:q, a:b]).then_inc(sem["tb%d" % c], 16)
+    load(0)
+
+    g.iota(T.dmp[:, :], [[16, 16]], DUMP, 1, allow_small_or_imprecise_dtypes=True).then_inc(sem.io_d, 1)
+    g.iota(T.pm[:, :], [[0, 8], [1, 16]], 0, -1, allow_small_or_imprecise_dtypes=True).then_inc(sem.io_p, 1)
+
+    fills = []
+
+    def fill(ap, c):
+        s = vs()
+        V.memset(ap, c).then_inc(s, 1)
+        fills.append(s)
+        return s
+
+    def op(call, *args, after=()):
+        for s in after:
+            V.wait_ge(s, 1)
+        s = vs()
+        call(*args).then_inc(s, 1)
+        return s
+    f_cf = fill(T.capf[:, 0:FB], BIG)
+    f_ep = fill(T.ep[0:1, 0:4], 0)
+    s_sel = op(V.tensor_scalar, T.sel[:, :], T.pm[:, :], 0.0, None, A.is_equal, after=[sem.io_p])
+    f_pads = [fill(T.win[:, a:a + PAD], -BIG) for a in (0, PAD + R, W - PAD)]
+
+    S.wait_ge(f_cf, 1)
+    for a in range(FB, NL, FB):
+        fills.append(ss())
+        S.activation(T.capf[:, a:a + FB], T.capf[:, 0:FB], COPY).then_inc(fills[-1], 1)
+
+    V.wait_ge(sem.ldi, 128)
+    s_l1 = op(V.tensor_scalar, T.lo[:, 0:HC], T.ix[:, 0:HC], float(PAD - far * R), float(PAD + R), A.add, A.min)
+    s_lo = op(V.tensor_scalar, T.lo[:, HC:2 * HC], T.ix[:, 0:HC], float(PAD - fmate * R), float(PAD + R), A.add, A.min)
+
+    V.wait_ge(sem.lde, 48)
+    eq = op(V.tensor_tensor, T.eq[:, :], T.en[:, :], T.ep[:, 3:19], A.is_equal, after=[f_ep])
+    x1 = op(V.tensor_scalar, T.x1[:, :], T.en[:, :], float(H), -1.0, A.min, A.add)
+    q2 = op(V.tensor_scalar, T.q2[:, :], T.ep[:, 3:19], float(H), float(H), A.is_ge, A.mult)
+    t1 = op(V.tensor_tensor, T.t1[:, :], T.eq[:, :], T.dmp[:, :], A.mult, after=[sem.io_d, eq])
+    t2 = op(V.tensor_scalar, T.ta[:, 0:WC], T.ix[:, HC:256], float(fbase + R), float(PAD), A.is_ge, A.mult)
+    st = op(V.tensor_tensor, T.pk[:, 16:32], T.en[:, :], T.t1[:, :], A.max, after=[t1])
+    u1 = op(V.tensor_tensor, T.u1[:, :], T.q2[:, :], T.t1[:, :], A.max, after=[q2])
+    t3 = op(V.tensor_tensor, T.tz[:, 0:WC], T.ta[:, 0:WC], T.ix[:, HC:256], A.add, after=[t2])
+    ga = op(V.tensor_scalar, T.pk[:, 0:16], T.pk[:, 16:32], float(DUMP), -1.0, A.min, A.add, after=[st])
+    Y.wait_ge(ga, 1)
+    load(1)
+    u2 = op(V.tensor_tensor, T.u2[:, :], T.u1[:, :], T.x1[:, :], A.max, after=[u1, x1])
+    gh = op(V.tensor_scalar, T.pk[:, 32:48], T.u2[:, :], float(H), None, A.min, after=[u2])
+    g.tensor.wait_ge(s_sel, 1)
+    for s in (st, ga, gh):
+        g.tensor.wait_ge(s, 1)
+    g.tensor.matmul(T.ps[:, :], T.sel[:, :], T.pk[:, :], True, True).then_inc(sem.pe, 1)
+    s_ow = op(V.tensor_scalar, T.eo[:, 0:WC], T.tz[:, 0:WC], float(PAD - fbase), float(2 * PAD + 2 * R), A.add, A.min, after=[t3])
+    s_eo = op(V.tensor_copy, T.eo[:, WC:WC + 48], T.ps[:, :], after=[sem.pe])
+    t4 = op(V.tensor_scalar, T.tc[:, :], T.ix[:, :], float(base + R), float(PAD), A.is_ge, A.mult)
+    Y.wait_ge(t4, 1)
+    load(2)
+    t5 = op(V.tensor_tensor, T.td[:, :], T.tc[:, :], T.ix[:, :], A.add, after=[t4])
+    s_oo = op(V.tensor_scalar, T.oo[:, :], T.td[:, :], float(PAD - base), float(2 * PAD + 2 * R), A.add, A.min, after=[t5])
+    fill(T.neg[:, :], -BIG)
+    fill(T.sd[:, H:H + 8], -BIG)
+    fill(T.sf[:, NL:NL + 8], 0.0)
+    fill(T.so[:, NL:NL + 8], 0.0)
+    fill(T.capf[:, NL:CAPW], BIG)
+    fill(T.capd[:, :], BIG)
+
+    sent = 0
+    g.wait_ge(s_l1, 1)
+    g.wait_ge(s_lo, 1)
+    sent += push(g, T, topo, core, out_relay, T.ml[:], T.lo[:], "lst")
+    g.wait_ge(s_ow, 1)
+    g.wait_ge(s_eo, 1)
+    sent += push(g, T, topo, core, out_relay, T.me[:], T.eo[:], "ends")
+    sent += push(g, T, topo, core, helper, T.he[:], T.eo[:, WC + 16:WC + 32], "hend")
+    for a, b, n in SWAPS:
+        for c in range(n):
+            g.wait_ge(sem["tb%d" % c], 16)
+        ap = T.win[:, mine + a:mine + b]
+        sent += push(g, T, topo, core, mcore, ap, ap, "mate")
+
+    n1, n2 = bits(topo.mask(in_relay, core)), bits(topo.mask(other_relay, core))
+    nm = len(SWAPS) * bits(topo.mask(mcore, core))
+    part, whole = T.win[:, low:low + PW], T.win[:, :]
+    for q in (V, S):
+        for c in range(len(LOADS)):
+            q.wait_ge(sem["tb%d" % c], 16)
+        for s in f_pads:
+            q.wait_ge(s, 1)
+
+    def vgather(out, window, off, a, b, col0=0):
+        return [(op(V.tensor_copy, out[:, a:b], window.indirect(off[:, a // 16 - col0:b // 16 - col0])), a, b)]
+
+    def sgather(out, window, off, cut, col0=0):
+        done = []
+        for a, b in zip(cut[:-1], cut[1:]):
+            s = ss()
+            S.activation(out[:, a:b], window.indirect(off[:, a // 16 - col0:b // 16 - col0]), COPY).then_inc(s, 1)
+            done.append((s, a, b))
+        return done
+
+    def scan(st, cap, gath, parts, prev=None):
+        for s_in, a, b in parts:
+            init = -BIG if prev is None else st[:, a - 1:a]
+            prev = op(V.tensor_tensor_scan, st[:, a:b], cap[:, a:b], gath[:, a:b], init, A.min, A.max,
+                      after=[s_in] + ([] if prev is None else [prev]))
+        return prev
+
+    S.wait_ge(sem.lst, n1)
+    p_c = sgather(T.gf, part, T.fl, SH)
+    S.wait_ge(sem.lsd, n2)
+    p_d = sgather(T.gd, part, T.fd, SH)
+    V.wait_ge(sem.lst, n1)
+    p_c = vgather(T.gf, part, T.fl, 0, VH) + p_c
+    V.wait_ge(sem.lsd, n2)
+    p_d = vgather(T.gd, part, T.fd, 0, VH) + p_d
+    for s in fills:
+        V.wait_ge(s, 1)
+    V.wait_ge(sem.end2, n2)
+    c_d = op(V.tensor_copy, T.capd[:, :].indirect(T.de[:, 0:16]), T.neg[:, :])
+    V.wait_ge(sem.ends, n1)
+    c_f = op(V.tensor_copy, T.capf[:, :].indirect(T.fe[:, WC + 16:WC + 32]), T.neg[:, :])
+    V.wait_ge(c_d, 1)
+    e_d = scan(T.sd, T.capd, T.gd, p_d)
+    s_pd = op(V.tensor_copy, T.pd[:, :], T.sd[:, :].indirect(T.de[:, 16:32]), after=[e_d])
+    g.wait_ge(s_pd, 1)
+    sent += push(g, T, topo, core, mcore, T.pm2[:], T.pd[:], "half")
+    V.wait_ge(c_f, 1)
+    e_c = scan(T.sf, T.capf, T.gf, p_c)
+
+    S.wait_ge(sem.mate, nm)
+    S.wait_ge(sem.ends, n1)
+    p_c = sgather(T.gf, whole, T.fe, SF, HC)
+    S.wait_ge(s_oo, 1)
+    p_o = sgather(T.go, whole, T.oo, SO)
+    V.wait_ge(sem.mate, nm)
+    p_c = vgather(T.gf, whole, T.fe, H, VF, HC) + p_c
+    e_c = scan(T.sf, T.capf, T.gf, p_c, e_c)
+    V.wait_ge(sem.half, bits(topo.mask(mcore, core)))
+    s_pf = op(V.tensor_tensor, T.pf[:, :], T.sf[:, :].indirect(T.fe[:, WC:WC + 16]), T.pm2[:, :], A.max, after=[e_c])
+    g.wait_ge(s_pf, 1)
+    sent += push(g, T, topo, core, in_relay, T.pr[:, 0:HB], T.pf[:, 0:HB], "prt0")
+    sent += push(g, T, topo, core, out_relay, T.pr[:, HB:NB], T.pf[:, HB:NB], "prt1")
+
+    V.wait_ge(s_oo, 1)
+    V.wait_ge(s_eo, 1)
+    p_o = vgather(T.go, whole, T.oo, 0, VO) + p_o
+    V.wait_ge(sem.ocap, bits(topo.mask(helper, core)))
+    e_o = scan(T.so, T.capo, T.go, p_o)
+    V.wait_ge(sem.fin, n1 + bits(topo.mask(out_relay, core)))
+    s_y = op(V.tensor_tensor, T.yo[:, :], T.so[:, :].indirect(T.eo[:, WC:WC + 16]), T.ph[:, :], A.max, after=[e_o])
+    Y.wait_ge(s_y, 1)
+    Y.dma_start(T.y[:, :], T.yo[:, :]).then_inc(sem.sty, 16)
+    Y.wait_ge(sem.sty, 16)
+    g.wait_ge(sem.sent, sent)

@@ -2,28 +2,17 @@ import numpy as np
 from concourse.mybir import dt, AluOpType, ActivationFunctionType
 
 R, NL, NB = 8192, 4096, 256
+HB = NB // 2
 PAD = 8
-W = 3 * PAD + 2 * R
-PW = R + 2 * PAD
+W = PAD + 2 * R + PAD
 BIG = float(201 * 2.0 ** 92)
 ZC = NL + 7
 DUMP = NL + 8
 CAPW = DUMP + NB
-H = 1536
-HC, WC = H // 16, (NL - H) // 16
-HB = NB // 2
-FB = 1024
-
-
-def cuts(a, b):
-    n = (b - a) // 32
-    return [a, a + 32 * (n // 2), a + 32 * (n * 4 // 5), b]
-
-
-VH, VF, VO = 320, H + 704, 1152
-SH, SF, SO = cuts(VH, H), cuts(VF, NL), cuts(VO, NL)
-LOADS = [(0, 128, 0, 4096), (0, 64, 4096, 8192), (64, 128, 4096, 8192)]
-SWAPS = [(0, 4096, 2), (4096, 8192, 3)]
+LOADS = [(0, 4096), (4096, 6144), (6144, 8192)]
+SWAPS = [(0, 4096, [0]), (4096, 8192, [1, 2])]
+FCUTS = [1280, 2432, 3456, 4096]
+OCUTS = [1024, 2432, 3456, 4096]
 
 SCRATCH = {
     "win": ("sbuf", [128, W], "bfloat16"),
@@ -35,48 +24,28 @@ SCRATCH = {
     "sel": ("sbuf", [16, 128], "float32"),
     "eq": ("sbuf", [16, 16], "float32"),
     "t1": ("sbuf", [16, 16], "float32"),
-    "q2": ("sbuf", [16, 16], "float32"),
-    "x1": ("sbuf", [16, 16], "float32"),
-    "u1": ("sbuf", [16, 16], "float32"),
-    "u2": ("sbuf", [16, 16], "float32"),
-    "pk": ("sbuf", [16, 48], "float32"),
-    "ta": ("sbuf", [128, 256], "int32"),
-    "tz": ("sbuf", [128, 256], "int32"),
-    "tc": ("sbuf", [128, 256], "int32"),
-    "td": ("sbuf", [128, 256], "int32"),
-    "lo": ("sbuf", [128, 2 * HC], "uint16"),
-    "ml": ("sbuf", [128, 2 * HC], "uint16"),
-    "fl": ("sbuf", [128, HC], "uint16"),
-    "fd": ("sbuf", [128, HC], "uint16"),
-    "eo": ("sbuf", [128, WC + 48], "uint16"),
-    "me": ("sbuf", [128, WC + 48], "uint16"),
-    "fe": ("sbuf", [128, WC + 32], "uint16"),
-    "de": ("sbuf", [128, 32], "uint16"),
-    "he": ("sbuf", [128, 16], "uint16"),
+    "pk": ("sbuf", [16, 32], "float32"),
+    "lo": ("sbuf", [128, 256], "uint16"),
     "oo": ("sbuf", [128, 256], "uint16"),
+    "eo": ("sbuf", [128, 32], "uint16"),
+    "fl": ("sbuf", [128, 256], "uint16"),
+    "fe": ("sbuf", [128, 32], "uint16"),
     "neg": ("sbuf", [128, 256], "bfloat16"),
-    "cap": ("sbuf", [128, CAPW], "bfloat16"),
-    "capo": ("sbuf", [128, NL], "bfloat16"),
+    "capo": ("sbuf", [128, CAPW], "bfloat16"),
     "capf": ("sbuf", [128, CAPW], "bfloat16"),
-    "capd": ("sbuf", [128, CAPW], "bfloat16"),
     "go": ("sbuf", [128, NL], "bfloat16"),
     "gf": ("sbuf", [128, NL], "bfloat16"),
-    "gd": ("sbuf", [128, H], "bfloat16"),
     "so": ("sbuf", [128, NL + 8], "bfloat16"),
     "sf": ("sbuf", [128, NL + 8], "bfloat16"),
-    "sd": ("sbuf", [128, H + 8], "bfloat16"),
-    "pd": ("sbuf", [128, NB], "bfloat16"),
-    "pm2": ("sbuf", [128, NB], "bfloat16"),
     "pf": ("sbuf", [128, NB], "bfloat16"),
     "pr": ("sbuf", [128, NB], "bfloat16"),
     "ph": ("sbuf", [128, NB], "bfloat16"),
     "yo": ("sbuf", [128, NB], "bfloat16"),
-    "ps": ("psum", [128, 48], "float32"),
+    "ps": ("psum", [128, 32], "float32"),
 }
-NV, NS = 80, 20
-SEMAPHORES = (["ldi", "lde", "sty", "lst", "lsd", "ends", "end2", "hend", "ocap", "mate", "half", "prt0", "prt1",
-               "fin", "sent", "io_d", "io_p", "pe"]
-              + ["tb%d" % k for k in range(len(LOADS))] + ["sc%d" % k for k in range(NS)] + ["v%d" % k for k in range(NV)])
+NV = 48
+SEMAPHORES = (["ldi", "lde", "sty", "lst", "ends", "mate", "prt0", "prt1", "fin", "sent", "io_d", "io_p", "pe"]
+              + ["tb%d" % k for k in range(len(LOADS))] + ["sc%d" % k for k in range(8)] + ["v%d" % k for k in range(NV)])
 
 _plan = {}
 
@@ -87,20 +56,17 @@ def make_plan(T, topo):
     cores = list(T.cores)
     n = len(cores)
     allc = range(512)
-    chip = lambda c, x: topo.host(c) == topo.host(x) and topo.chip(c) == topo.chip(x)
-    here = lambda c, x: chip(c, x) and topo.die(c) == topo.die(x)
+    here = lambda c, x: topo.host(c) == topo.host(x) and topo.chip(c) == topo.chip(x) and topo.die(c) == topo.die(x)
     for i in range(n):
         r = cores[i]
-        mate = [j for j in range(n) if j != i and chip(cores[j], r)][0]
+        mate = [j for j in range(n) if j != i and topo.host(cores[j]) == topo.host(r) and topo.chip(cores[j]) == topo.chip(r)][0]
         far = [j for j in range(n) if topo.host(cores[j]) != topo.host(r) and topo.die(cores[j]) == topo.die(r)][0]
         f = cores[far]
-        fm = [c for c in cores if c != f and chip(c, f)][0]
         place = [c for c in allc if here(c, r)].index(r)
         rel = [c for c in allc if topo.host(c) not in (topo.host(r), topo.host(f))
                and topo.rack(topo.host(c)) == topo.rack(topo.host(r)) and topo.chip(c) == topo.chip(r) and topo.die(c) == topo.die(r)
-               and topo.may_write(r, c) and topo.may_write(c, f) and topo.may_write(c, fm) and topo.may_write(f, c) and topo.may_write(c, r)]
-        helper = [c for c in allc if here(c, r) and c not in cores][0]
-        _plan[i] = {"mate": mate, "far": far, "relay": rel[place], "helper": helper}
+               and topo.may_write(r, c) and topo.may_write(c, f) and topo.may_write(f, c) and topo.may_write(c, r)]
+        _plan[i] = {"mate": mate, "far": far, "relay": rel[place]}
     return _plan
 
 
@@ -115,31 +81,16 @@ def push(g, T, topo, core, dst, out, src, sem):
     return bits(m)
 
 
-def relay_program(g, core, T, topo, r, f, fm):
+def relay_program(g, core, T, topo, r, f):
     n = bits(topo.mask(r, core))
     g.wait_ge(T.sem.lst, n)
-    k = push(g, T, topo, core, f, T.fl[:], T.ml[:, 0:HC], "lst")
-    k += push(g, T, topo, core, fm, T.fd[:], T.ml[:, HC:2 * HC], "lsd")
+    k = push(g, T, topo, core, f, T.fl[:], T.fl[:], "lst")
     g.wait_ge(T.sem.ends, n)
-    k += push(g, T, topo, core, fm, T.de[:], T.me[:, WC + 16:WC + 48], "end2")
-    k += push(g, T, topo, core, f, T.fe[:], T.me[:, 0:WC + 32], "ends")
+    k += push(g, T, topo, core, f, T.fe[:], T.fe[:], "ends")
     g.wait_ge(T.sem.prt0, bits(topo.mask(f, core)))
     k += push(g, T, topo, core, r, T.ph[:, 0:HB], T.pr[:, 0:HB], "fin")
     g.wait_ge(T.sem.prt1, n)
     k += push(g, T, topo, core, f, T.ph[:, HB:NB], T.pr[:, HB:NB], "fin")
-    g.wait_ge(T.sem.sent, k)
-
-
-def helper_program(g, core, T, topo, r):
-    V = g.vector
-    V.memset(T.neg[:, :], -BIG).then_inc(T.sem.v0, 1)
-    V.memset(T.cap[:, :], BIG).then_inc(T.sem.v1, 1)
-    V.wait_ge(T.sem.v0, 1)
-    V.wait_ge(T.sem.v1, 1)
-    V.wait_ge(T.sem.hend, bits(topo.mask(r, core)))
-    V.tensor_copy(T.cap[:, :].indirect(T.he[:, :]), T.neg[:, :]).then_inc(T.sem.v2, 1)
-    g.wait_ge(T.sem.v2, 1)
-    k = push(g, T, topo, core, r, T.capo[:], T.cap[:, 0:NL], "ocap")
     g.wait_ge(T.sem.sent, k)
 
 
@@ -149,33 +100,23 @@ def rank_program(g, core, T, topo):
     rank = T.rank_of(core)
     if rank is None:
         for i in plan:
-            far = plan[i]["far"]
             if plan[i]["relay"] == core:
-                relay_program(g, core, T, topo, cores[i], cores[far], cores[plan[far]["mate"]])
-            if plan[i]["helper"] == core:
-                helper_program(g, core, T, topo, cores[i])
+                relay_program(g, core, T, topo, cores[i], cores[plan[i]["far"]])
         return
-    mate, far, helper = plan[rank]["mate"], plan[rank]["far"], plan[rank]["helper"]
-    fmate = plan[far]["mate"]
+    mate, far = plan[rank]["mate"], plan[rank]["far"]
     mcore = cores[mate]
-    out_relay, in_relay, other_relay = plan[rank]["relay"], plan[far]["relay"], plan[fmate]["relay"]
+    out_relay, in_relay = plan[rank]["relay"], plan[far]["relay"]
     base = R * min(rank, mate)
-    fbase = R * min(far, fmate)
-    low = (rank * R - base) // R * (R + PAD)
-    mine = low + PAD
+    fbase = R * min(far, plan[far]["mate"])
+    mine = PAD + R * rank - base
     V, S, Y = g.vector, g.scalar, g.sync
     sem = T.sem
     A = AluOpType
-    COPY = ActivationFunctionType.Copy
-    nv, ns = [0], [0]
+    cnt = [0]
 
     def vs():
-        nv[0] += 1
-        return sem["v%d" % (nv[0] - 1)]
-
-    def ss():
-        ns[0] += 1
-        return sem["sc%d" % (ns[0] - 1)]
+        cnt[0] += 1
+        return sem["v%d" % (cnt[0] - 1)]
 
     for k in range(4):
         Y.dma_start(T.ix[16 * k:16 * k + 16, :], T.idx[:, :]).then_inc(sem.ldi, 16)
@@ -185,10 +126,11 @@ def rank_program(g, core, T, topo):
     S.dma_start(T.ep[1:16, 3:19], T.end[0:15, :]).then_inc(sem.lde, 16)
     S.dma_start(T.ep[0:1, 4:19], T.end[15:16, 0:15]).then_inc(sem.lde, 16)
 
-    def load(c):
-        p, q, a, b = LOADS[c]
-        Y.dma_start(T.win[p:q, mine + a:mine + b], T.tab[p:q, a:b]).then_inc(sem["tb%d" % c], 16)
-    load(0)
+    def load(q, c):
+        a, b = LOADS[c]
+        q.dma_start(T.win[:, mine + a:mine + b], T.tab[:, a:b]).then_inc(sem["tb%d" % c], 16)
+    load(Y, 0)
+    load(S, 1)
 
     g.iota(T.dmp[:, :], [[16, 16]], DUMP, 1, allow_small_or_imprecise_dtypes=True).then_inc(sem.io_d, 1)
     g.iota(T.pm[:, :], [[0, 8], [1, 16]], 0, -1, allow_small_or_imprecise_dtypes=True).then_inc(sem.io_p, 1)
@@ -200,143 +142,120 @@ def rank_program(g, core, T, topo):
         V.memset(ap, c).then_inc(s, 1)
         fills.append(s)
         return s
-
-    def op(call, *args, after=()):
-        for s in after:
-            V.wait_ge(s, 1)
-        s = vs()
-        call(*args).then_inc(s, 1)
-        return s
-    f_cf = fill(T.capf[:, 0:FB], BIG)
+    fill(T.win[:, 0:PAD], -BIG)
+    fill(T.win[:, W - PAD:W], -BIG)
     f_ep = fill(T.ep[0:1, 0:4], 0)
-    s_sel = op(V.tensor_scalar, T.sel[:, :], T.pm[:, :], 0.0, None, A.is_equal, after=[sem.io_p])
-    f_pads = [fill(T.win[:, a:a + PAD], -BIG) for a in (0, PAD + R, W - PAD)]
+    fill(T.neg[:, :], -BIG)
+    s_eq, s_t1, s_st, s_ga, s_sel, s_eo = vs(), vs(), vs(), vs(), vs(), vs()
+    V.wait_ge(sem.io_p, 1)
+    V.tensor_scalar(T.sel[:, :], T.pm[:, :], 0.0, None, A.is_equal).then_inc(s_sel, 1)
 
-    S.wait_ge(f_cf, 1)
-    for a in range(FB, NL, FB):
-        fills.append(ss())
-        S.activation(T.capf[:, a:a + FB], T.capf[:, 0:FB], COPY).then_inc(fills[-1], 1)
-
+    def offsets(out, b):
+        s = vs()
+        if b == 0:
+            V.tensor_scalar(out, T.ix[:, :], float(PAD), float(PAD + 2 * R), A.add, A.min).then_inc(s, 1)
+        else:
+            V.tensor_scalar(out, T.ix[:, :], float(PAD - b), float(PAD - 1), A.add, A.max).then_inc(s, 1)
+        return s
     V.wait_ge(sem.ldi, 128)
-    s_l1 = op(V.tensor_scalar, T.lo[:, 0:HC], T.ix[:, 0:HC], float(PAD - far * R), float(PAD + R), A.add, A.min)
-    s_lo = op(V.tensor_scalar, T.lo[:, HC:2 * HC], T.ix[:, 0:HC], float(PAD - fmate * R), float(PAD + R), A.add, A.min)
+    s_lo = offsets(T.lo[:, :], fbase)
+    Y.wait_ge(s_lo, 1)
+    load(Y, 2)
 
     V.wait_ge(sem.lde, 48)
-    eq = op(V.tensor_tensor, T.eq[:, :], T.en[:, :], T.ep[:, 3:19], A.is_equal, after=[f_ep])
-    x1 = op(V.tensor_scalar, T.x1[:, :], T.en[:, :], float(H), -1.0, A.min, A.add)
-    q2 = op(V.tensor_scalar, T.q2[:, :], T.ep[:, 3:19], float(H), float(H), A.is_ge, A.mult)
-    t1 = op(V.tensor_tensor, T.t1[:, :], T.eq[:, :], T.dmp[:, :], A.mult, after=[sem.io_d, eq])
-    t2 = op(V.tensor_scalar, T.ta[:, 0:WC], T.ix[:, HC:256], float(fbase + R), float(PAD), A.is_ge, A.mult)
-    st = op(V.tensor_tensor, T.pk[:, 16:32], T.en[:, :], T.t1[:, :], A.max, after=[t1])
-    u1 = op(V.tensor_tensor, T.u1[:, :], T.q2[:, :], T.t1[:, :], A.max, after=[q2])
-    t3 = op(V.tensor_tensor, T.tz[:, 0:WC], T.ta[:, 0:WC], T.ix[:, HC:256], A.add, after=[t2])
-    ga = op(V.tensor_scalar, T.pk[:, 0:16], T.pk[:, 16:32], float(DUMP), -1.0, A.min, A.add, after=[st])
-    Y.wait_ge(ga, 1)
-    load(1)
-    u2 = op(V.tensor_tensor, T.u2[:, :], T.u1[:, :], T.x1[:, :], A.max, after=[u1, x1])
-    gh = op(V.tensor_scalar, T.pk[:, 32:48], T.u2[:, :], float(H), None, A.min, after=[u2])
+    V.wait_ge(f_ep, 1)
+    V.tensor_tensor(T.eq[:, :], T.en[:, :], T.ep[:, 3:19], A.is_equal).then_inc(s_eq, 1)
+    V.wait_ge(sem.io_d, 1)
+    V.wait_ge(s_eq, 1)
+    V.tensor_tensor(T.t1[:, :], T.eq[:, :], T.dmp[:, :], A.mult).then_inc(s_t1, 1)
+    V.wait_ge(s_t1, 1)
+    V.tensor_tensor(T.pk[:, 0:16], T.en[:, :], T.t1[:, :], A.max).then_inc(s_st, 1)
+    V.wait_ge(s_st, 1)
+    V.tensor_scalar(T.pk[:, 16:32], T.pk[:, 0:16], float(DUMP), -1.0, A.min, A.add).then_inc(s_ga, 1)
     g.tensor.wait_ge(s_sel, 1)
-    for s in (st, ga, gh):
-        g.tensor.wait_ge(s, 1)
+    g.tensor.wait_ge(s_ga, 1)
     g.tensor.matmul(T.ps[:, :], T.sel[:, :], T.pk[:, :], True, True).then_inc(sem.pe, 1)
-    s_ow = op(V.tensor_scalar, T.eo[:, 0:WC], T.tz[:, 0:WC], float(PAD - fbase), float(2 * PAD + 2 * R), A.add, A.min, after=[t3])
-    s_eo = op(V.tensor_copy, T.eo[:, WC:WC + 48], T.ps[:, :], after=[sem.pe])
-    t4 = op(V.tensor_scalar, T.tc[:, :], T.ix[:, :], float(base + R), float(PAD), A.is_ge, A.mult)
-    Y.wait_ge(t4, 1)
-    load(2)
-    t5 = op(V.tensor_tensor, T.td[:, :], T.tc[:, :], T.ix[:, :], A.add, after=[t4])
-    s_oo = op(V.tensor_scalar, T.oo[:, :], T.td[:, :], float(PAD - base), float(2 * PAD + 2 * R), A.add, A.min, after=[t5])
-    fill(T.neg[:, :], -BIG)
-    fill(T.sd[:, H:H + 8], -BIG)
-    fill(T.sf[:, NL:NL + 8], 0.0)
+    V.wait_ge(sem.pe, 1)
+    V.tensor_copy(T.eo[:, :], T.ps[:, :]).then_inc(s_eo, 1)
+    s_oo = offsets(T.oo[:, :], base)
     fill(T.so[:, NL:NL + 8], 0.0)
-    fill(T.capf[:, NL:CAPW], BIG)
-    fill(T.capd[:, :], BIG)
+    fill(T.sf[:, NL:NL + 8], 0.0)
+    fill(T.capf[:, :], BIG)
+    fill(T.capo[:, :], BIG)
+    for s in fills:
+        V.wait_ge(s, 1)
+
+    def scatter(cap, off):
+        s = vs()
+        V.tensor_copy(cap[:, :].indirect(off[:, 0:16]), T.neg[:, :]).then_inc(s, 1)
+        return s
+    V.wait_ge(s_eo, 1)
+    c_own = scatter(T.capo, T.eo)
 
     sent = 0
-    g.wait_ge(s_l1, 1)
     g.wait_ge(s_lo, 1)
-    sent += push(g, T, topo, core, out_relay, T.ml[:], T.lo[:], "lst")
-    g.wait_ge(s_ow, 1)
+    sent += push(g, T, topo, core, out_relay, T.fl[:], T.lo[:], "lst")
     g.wait_ge(s_eo, 1)
-    sent += push(g, T, topo, core, out_relay, T.me[:], T.eo[:], "ends")
-    sent += push(g, T, topo, core, helper, T.he[:], T.eo[:, WC + 16:WC + 32], "hend")
-    for a, b, n in SWAPS:
-        for c in range(n):
+    sent += push(g, T, topo, core, out_relay, T.fe[:], T.eo[:], "ends")
+    for a, b, need in SWAPS:
+        for c in need:
             g.wait_ge(sem["tb%d" % c], 16)
         ap = T.win[:, mine + a:mine + b]
         sent += push(g, T, topo, core, mcore, ap, ap, "mate")
 
-    n1, n2 = bits(topo.mask(in_relay, core)), bits(topo.mask(other_relay, core))
     nm = len(SWAPS) * bits(topo.mask(mcore, core))
-    part, whole = T.win[:, low:low + PW], T.win[:, :]
+    nl = bits(topo.mask(in_relay, core))
+    V.wait_ge(sem.ends, nl)
+    c_far = scatter(T.capf, T.fe)
+
     for q in (V, S):
+        q.wait_ge(sem.lst, nl)
         for c in range(len(LOADS)):
             q.wait_ge(sem["tb%d" % c], 16)
-        for s in f_pads:
-            q.wait_ge(s, 1)
+        q.wait_ge(sem.mate, nm)
+    for s in fills[:2]:
+        S.wait_ge(s, 1)
+    S.wait_ge(s_oo, 1)
+    nsc = [0]
 
-    def vgather(out, window, off, a, b, col0=0):
-        return [(op(V.tensor_copy, out[:, a:b], window.indirect(off[:, a // 16 - col0:b // 16 - col0])), a, b)]
-
-    def sgather(out, window, off, cut, col0=0):
+    def sgather(out, off, cuts):
         done = []
-        for a, b in zip(cut[:-1], cut[1:]):
-            s = ss()
-            S.activation(out[:, a:b], window.indirect(off[:, a // 16 - col0:b // 16 - col0]), COPY).then_inc(s, 1)
+        for a, b in zip(cuts[:-1], cuts[1:]):
+            s = sem["sc%d" % nsc[0]]
+            nsc[0] += 1
+            S.activation(out[:, a:b], T.win[:, :].indirect(off[:, a // 16:b // 16]), ActivationFunctionType.Copy).then_inc(s, 1)
             done.append((s, a, b))
         return done
+    part_f = sgather(T.gf, T.fl, FCUTS)
+    part_o = sgather(T.go, T.oo, OCUTS)
 
-    def scan(st, cap, gath, parts, prev=None):
-        for s_in, a, b in parts:
+    def states(gath, st, cap, c_done, off, parts):
+        v = parts[0][1]
+        s = vs()
+        V.tensor_copy(gath[:, 0:v], T.win[:, :].indirect(off[:, 0:v // 16])).then_inc(s, 1)
+        V.wait_ge(c_done, 1)
+        prev = None
+        for s_in, a, b in [(s, 0, v)] + parts:
+            V.wait_ge(s_in, 1)
+            if prev is not None:
+                V.wait_ge(prev, 1)
             init = -BIG if prev is None else st[:, a - 1:a]
-            prev = op(V.tensor_tensor_scan, st[:, a:b], cap[:, a:b], gath[:, a:b], init, A.min, A.max,
-                      after=[s_in] + ([] if prev is None else [prev]))
-        return prev
+            prev = vs()
+            V.tensor_tensor_scan(st[:, a:b], cap[:, a:b], gath[:, a:b], init, A.min, A.max).then_inc(prev, 1)
+        V.wait_ge(prev, 1)
 
-    S.wait_ge(sem.lst, n1)
-    p_c = sgather(T.gf, part, T.fl, SH)
-    S.wait_ge(sem.lsd, n2)
-    p_d = sgather(T.gd, part, T.fd, SH)
-    V.wait_ge(sem.lst, n1)
-    p_c = vgather(T.gf, part, T.fl, 0, VH) + p_c
-    V.wait_ge(sem.lsd, n2)
-    p_d = vgather(T.gd, part, T.fd, 0, VH) + p_d
-    for s in fills:
-        V.wait_ge(s, 1)
-    V.wait_ge(sem.end2, n2)
-    c_d = op(V.tensor_copy, T.capd[:, :].indirect(T.de[:, 0:16]), T.neg[:, :])
-    V.wait_ge(sem.ends, n1)
-    c_f = op(V.tensor_copy, T.capf[:, :].indirect(T.fe[:, WC + 16:WC + 32]), T.neg[:, :])
-    V.wait_ge(c_d, 1)
-    e_d = scan(T.sd, T.capd, T.gd, p_d)
-    s_pd = op(V.tensor_copy, T.pd[:, :], T.sd[:, :].indirect(T.de[:, 16:32]), after=[e_d])
-    g.wait_ge(s_pd, 1)
-    sent += push(g, T, topo, core, mcore, T.pm2[:], T.pd[:], "half")
-    V.wait_ge(c_f, 1)
-    e_c = scan(T.sf, T.capf, T.gf, p_c)
-
-    S.wait_ge(sem.mate, nm)
-    S.wait_ge(sem.ends, n1)
-    p_c = sgather(T.gf, whole, T.fe, SF, HC)
-    S.wait_ge(s_oo, 1)
-    p_o = sgather(T.go, whole, T.oo, SO)
-    V.wait_ge(sem.mate, nm)
-    p_c = vgather(T.gf, whole, T.fe, H, VF, HC) + p_c
-    e_c = scan(T.sf, T.capf, T.gf, p_c, e_c)
-    V.wait_ge(sem.half, bits(topo.mask(mcore, core)))
-    s_pf = op(V.tensor_tensor, T.pf[:, :], T.sf[:, :].indirect(T.fe[:, WC:WC + 16]), T.pm2[:, :], A.max, after=[e_c])
+    states(T.gf, T.sf, T.capf, c_far, T.fl, part_f)
+    s_pf = vs()
+    V.tensor_copy(T.pf[:, :], T.sf[:, :].indirect(T.fe[:, 16:32])).then_inc(s_pf, 1)
     g.wait_ge(s_pf, 1)
     sent += push(g, T, topo, core, in_relay, T.pr[:, 0:HB], T.pf[:, 0:HB], "prt0")
     sent += push(g, T, topo, core, out_relay, T.pr[:, HB:NB], T.pf[:, HB:NB], "prt1")
 
     V.wait_ge(s_oo, 1)
-    V.wait_ge(s_eo, 1)
-    p_o = vgather(T.go, whole, T.oo, 0, VO) + p_o
-    V.wait_ge(sem.ocap, bits(topo.mask(helper, core)))
-    e_o = scan(T.so, T.capo, T.go, p_o)
-    V.wait_ge(sem.fin, n1 + bits(topo.mask(out_relay, core)))
-    s_y = op(V.tensor_tensor, T.yo[:, :], T.so[:, :].indirect(T.eo[:, WC:WC + 16]), T.ph[:, :], A.max, after=[e_o])
+    states(T.go, T.so, T.capo, c_own, T.oo, part_o)
+    V.wait_ge(sem.fin, nl + bits(topo.mask(out_relay, core)))
+    s_y = vs()
+    V.tensor_tensor(T.yo[:, :], T.so[:, :].indirect(T.eo[:, 16:32]), T.ph[:, :], A.max).then_inc(s_y, 1)
     Y.wait_ge(s_y, 1)
     Y.dma_start(T.y[:, :], T.yo[:, :]).then_inc(sem.sty, 16)
     Y.wait_ge(sem.sty, 16)

@@ -9,9 +9,9 @@ BIG = float(201 * 2.0 ** 92)
 ZC = NL + 7
 DUMP = NL + 8
 CAPW = DUMP + NB
-LOADS = [(0, 4096), (4096, 6144), (6144, 8192)]
-SWAPS = [(0, 4096, [0]), (4096, 8192, [1, 2])]
-FCUTS = [1280, 2432, 3456, 4096]
+LOADS = [(0, 4096), (4096, 8192)]
+SWAPS = [(0, 4096, [0]), (4096, 8192, [1])]
+FCUTS = [1280, 2048, 3328, 4096]
 OCUTS = [1024, 2432, 3456, 4096]
 
 SCRATCH = {
@@ -29,6 +29,7 @@ SCRATCH = {
     "oo": ("sbuf", [128, 256], "uint16"),
     "eo": ("sbuf", [128, 32], "uint16"),
     "fl": ("sbuf", [128, 256], "uint16"),
+    "rl": ("sbuf", [128, 256], "uint16"),
     "fe": ("sbuf", [128, 32], "uint16"),
     "neg": ("sbuf", [128, 256], "bfloat16"),
     "capo": ("sbuf", [128, CAPW], "bfloat16"),
@@ -44,7 +45,7 @@ SCRATCH = {
     "ps": ("psum", [128, 32], "float32"),
 }
 NV = 48
-SEMAPHORES = (["ldi", "lde", "sty", "lst", "ends", "mate", "prt0", "prt1", "fin", "sent", "io_d", "io_p", "pe"]
+SEMAPHORES = (["ldi", "lde", "sty", "ls0", "ls1", "ends", "mate", "prt0", "prt1", "fin", "sent", "io_d", "io_p", "pe"]
               + ["tb%d" % k for k in range(len(LOADS))] + ["sc%d" % k for k in range(8)] + ["v%d" % k for k in range(NV)])
 
 _plan = {}
@@ -82,12 +83,14 @@ def push(g, T, topo, core, dst, out, src, sem):
 
 
 def relay_program(g, core, T, topo, r, f):
-    n = bits(topo.mask(r, core))
-    g.wait_ge(T.sem.lst, n)
-    k = push(g, T, topo, core, f, T.fl[:], T.fl[:], "lst")
+    n, m = bits(topo.mask(r, core)), bits(topo.mask(f, core))
+    g.wait_ge(T.sem.ls0, n)
+    k = push(g, T, topo, core, f, T.fl[:, 0:128], T.rl[:, 0:128], "ls0")
+    g.wait_ge(T.sem.ls1, m)
+    k += push(g, T, topo, core, r, T.fl[:, 128:256], T.rl[:, 128:256], "ls1")
     g.wait_ge(T.sem.ends, n)
     k += push(g, T, topo, core, f, T.fe[:], T.fe[:], "ends")
-    g.wait_ge(T.sem.prt0, bits(topo.mask(f, core)))
+    g.wait_ge(T.sem.prt0, m)
     k += push(g, T, topo, core, r, T.ph[:, 0:HB], T.pr[:, 0:HB], "fin")
     g.wait_ge(T.sem.prt1, n)
     k += push(g, T, topo, core, f, T.ph[:, HB:NB], T.pr[:, HB:NB], "fin")
@@ -130,7 +133,6 @@ def rank_program(g, core, T, topo):
         a, b = LOADS[c]
         q.dma_start(T.win[:, mine + a:mine + b], T.tab[:, a:b]).then_inc(sem["tb%d" % c], 16)
     load(Y, 0)
-    load(S, 1)
 
     g.iota(T.dmp[:, :], [[16, 16]], DUMP, 1, allow_small_or_imprecise_dtypes=True).then_inc(sem.io_d, 1)
     g.iota(T.pm[:, :], [[0, 8], [1, 16]], 0, -1, allow_small_or_imprecise_dtypes=True).then_inc(sem.io_p, 1)
@@ -160,7 +162,7 @@ def rank_program(g, core, T, topo):
     V.wait_ge(sem.ldi, 128)
     s_lo = offsets(T.lo[:, :], fbase)
     Y.wait_ge(s_lo, 1)
-    load(Y, 2)
+    load(Y, 1)
 
     V.wait_ge(sem.lde, 48)
     V.wait_ge(f_ep, 1)
@@ -194,7 +196,8 @@ def rank_program(g, core, T, topo):
 
     sent = 0
     g.wait_ge(s_lo, 1)
-    sent += push(g, T, topo, core, out_relay, T.fl[:], T.lo[:], "lst")
+    sent += push(g, T, topo, core, out_relay, T.rl[:, 0:128], T.lo[:, 0:128], "ls0")
+    sent += push(g, T, topo, core, in_relay, T.rl[:, 128:256], T.lo[:, 128:256], "ls1")
     g.wait_ge(s_eo, 1)
     sent += push(g, T, topo, core, out_relay, T.fe[:], T.eo[:], "ends")
     for a, b, need in SWAPS:
@@ -204,17 +207,18 @@ def rank_program(g, core, T, topo):
         sent += push(g, T, topo, core, mcore, ap, ap, "mate")
 
     nm = len(SWAPS) * bits(topo.mask(mcore, core))
-    nl = bits(topo.mask(in_relay, core))
+    nl, no = bits(topo.mask(in_relay, core)), bits(topo.mask(out_relay, core))
     V.wait_ge(sem.ends, nl)
     c_far = scatter(T.capf, T.fe)
 
     for q in (V, S):
-        q.wait_ge(sem.lst, nl)
+        q.wait_ge(sem.ls0, nl)
         for c in range(len(LOADS)):
             q.wait_ge(sem["tb%d" % c], 16)
         q.wait_ge(sem.mate, nm)
     for s in fills[:2]:
         S.wait_ge(s, 1)
+    S.wait_ge(sem.ls1, no)
     S.wait_ge(s_oo, 1)
     nsc = [0]
 
@@ -253,7 +257,7 @@ def rank_program(g, core, T, topo):
 
     V.wait_ge(s_oo, 1)
     states(T.go, T.so, T.capo, c_own, T.oo, part_o)
-    V.wait_ge(sem.fin, nl + bits(topo.mask(out_relay, core)))
+    V.wait_ge(sem.fin, nl + no)
     s_y = vs()
     V.tensor_tensor(T.yo[:, :], T.so[:, :].indirect(T.eo[:, 16:32]), T.ph[:, :], A.max).then_inc(s_y, 1)
     Y.wait_ge(s_y, 1)

import numpy as np
from concourse.mybir import dt, AluOpType, ActivationFunctionType

R, NL, NB = 8192, 4096, 256
HB = NB // 2
PAD = 8
W = PAD + 2 * R + PAD
BIG = float(201 * 2.0 ** 92)
ZC = NL + 7
DUMP = NL + 8
CAPW = DUMP + NB
LOADS = [(0, 4096), (4096, 8192)]
SWAPS = [(0, 4096, [0]), (4096, 8192, [1])]
FCUTS = [1280, 2048, 3328, 4096]
OCUTS = [1024, 2432, 3456, 4096]

SCRATCH = {
    "win": ("sbuf", [128, W], "bfloat16"),
    "ix": ("sbuf", [128, 256], "int32"),
    "en": ("sbuf", [16, 16], "int32"),
    "ep": ("sbuf", [16, 20], "int32"),
    "dmp": ("sbuf", [16, 16], "float32"),
    "pm": ("sbuf", [16, 128], "float32"),
    "sel": ("sbuf", [16, 128], "float32"),
    "eq": ("sbuf", [16, 16], "float32"),
    "t1": ("sbuf", [16, 16], "float32"),
    "pk": ("sbuf", [16, 32], "float32"),
    "lo": ("sbuf", [128, 256], "uint16"),
    "oo": ("sbuf", [128, 256], "uint16"),
    "eo": ("sbuf", [128, 32], "uint16"),
    "fl": ("sbuf", [128, 256], "uint16"),
    "rl": ("sbuf", [128, 256], "uint16"),
    "fe": ("sbuf", [128, 32], "uint16"),
    "neg": ("sbuf", [128, 256], "bfloat16"),
    "capo": ("sbuf", [128, CAPW], "bfloat16"),
    "capf": ("sbuf", [128, CAPW], "bfloat16"),
    "go": ("sbuf", [128, NL], "bfloat16"),
    "gf": ("sbuf", [128, NL], "bfloat16"),
    "so": ("sbuf", [128, NL + 8], "bfloat16"),
    "sf": ("sbuf", [128, NL + 8], "bfloat16"),
    "pf": ("sbuf", [128, NB], "bfloat16"),
    "pr": ("sbuf", [128, NB], "bfloat16"),
    "ph": ("sbuf", [128, NB], "bfloat16"),
    "yo": ("sbuf", [128, NB], "bfloat16"),
    "ps": ("psum", [128, 32], "float32"),
}
NV = 48
SEMAPHORES = (["ldi", "lde", "sty", "ls0", "ls1", "ends", "mate", "prt0", "prt1", "fin", "sent", "io_d", "io_p", "pe"]
              + ["tb%d" % k for k in range(len(LOADS))] + ["sc%d" % k for k in range(8)] + ["v%d" % k for k in range(NV)])

_plan = {}


def make_plan(T, topo):
    if _plan:
        return _plan
    cores = list(T.cores)
    n = len(cores)
    allc = range(512)
    here = lambda c, x: topo.host(c) == topo.host(x) and topo.chip(c) == topo.chip(x) and topo.die(c) == topo.die(x)
    for i in range(n):
        r = cores[i]
        mate = [j for j in range(n) if j != i and topo.host(cores[j]) == topo.host(r) and topo.chip(cores[j]) == topo.chip(r)][0]
        far = [j for j in range(n) if topo.host(cores[j]) != topo.host(r) and topo.die(cores[j]) == topo.die(r)][0]
        f = cores[far]
        place = [c for c in allc if here(c, r)].index(r)
        rel = [c for c in allc if topo.host(c) not in (topo.host(r), topo.host(f))
               and topo.rack(topo.host(c)) == topo.rack(topo.host(r)) and topo.chip(c) == topo.chip(r) and topo.die(c) == topo.die(r)
               and topo.may_write(r, c) and topo.may_write(c, f) and topo.may_write(f, c) and topo.may_write(c, r)]
        _plan[i] = {"mate": mate, "far": far, "relay": rel[place]}
    return _plan


def bits(m):
    return bin(m).count("1")


def push(g, T, topo, core, dst, out, src, sem):
    rid, pid = topo.addr(dst, core)
    m = topo.mask(core, dst)
    g.remote_dma(out, src, T.sem[sem], T.sem.sent, pid, rid, m)
    return bits(m)


def relay_program(g, core, T, topo, r, f):
    n, m = bits(topo.mask(r, core)), bits(topo.mask(f, core))
    g.wait_ge(T.sem.ls0, n)
    k = push(g, T, topo, core, f, T.fl[:, 0:128], T.rl[:, 0:128], "ls0")
    g.wait_ge(T.sem.ls1, m)
    k += push(g, T, topo, core, r, T.fl[:, 128:256], T.rl[:, 128:256], "ls1")
    g.wait_ge(T.sem.ends, n)
    k += push(g, T, topo, core, f, T.fe[:], T.fe[:], "ends")
    g.wait_ge(T.sem.prt0, m)
    k += push(g, T, topo, core, r, T.ph[:, 0:HB], T.pr[:, 0:HB], "fin")
    g.wait_ge(T.sem.prt1, n)
    k += push(g, T, topo, core, f, T.ph[:, HB:NB], T.pr[:, HB:NB], "fin")
    g.wait_ge(T.sem.sent, k)


def rank_program(g, core, T, topo):
    plan = make_plan(T, topo)
    cores = list(T.cores)
    rank = T.rank_of(core)
    if rank is None:
        for i in plan:
            if plan[i]["relay"] == core:
                relay_program(g, core, T, topo, cores[i], cores[plan[i]["far"]])
        return
    mate, far = plan[rank]["mate"], plan[rank]["far"]
    mcore = cores[mate]
    out_relay, in_relay = plan[rank]["relay"], plan[far]["relay"]
    base = R * min(rank, mate)
    fbase = R * min(far, plan[far]["mate"])
    mine = PAD + R * rank - base
    V, S, Y = g.vector, g.scalar, g.sync
    sem = T.sem
    A = AluOpType
    cnt = [0]

    def vs():
        cnt[0] += 1
        return sem["v%d" % (cnt[0] - 1)]

    for k in range(4):
        Y.dma_start(T.ix[16 * k:16 * k + 16, :], T.idx[:, :]).then_inc(sem.ldi, 16)
    for k in range(4, 8):
        S.dma_start(T.ix[16 * k:16 * k + 16, :], T.idx[:, :]).then_inc(sem.ldi, 16)
    Y.dma_start(T.en[:, :], T.end[:, :]).then_inc(sem.lde, 16)
    S.dma_start(T.ep[1:16, 3:19], T.end[0:15, :]).then_inc(sem.lde, 16)
    S.dma_start(T.ep[0:1, 4:19], T.end[15:16, 0:15]).then_inc(sem.lde, 16)

    def load(q, c):
        a, b = LOADS[c]
        q.dma_start(T.win[:, mine + a:mine + b], T.tab[:, a:b]).then_inc(sem["tb%d" % c], 16)
    load(Y, 0)

    g.iota(T.dmp[:, :], [[16, 16]], DUMP, 1, allow_small_or_imprecise_dtypes=True).then_inc(sem.io_d, 1)
    g.iota(T.pm[:, :], [[0, 8], [1, 16]], 0, -1, allow_small_or_imprecise_dtypes=True).then_inc(sem.io_p, 1)

    fills = []

    def fill(ap, c):
        s = vs()
        V.memset(ap, c).then_inc(s, 1)
        fills.append(s)
        return s
    fill(T.win[:, 0:PAD], -BIG)
    fill(T.win[:, W - PAD:W], -BIG)
    f_ep = fill(T.ep[0:1, 0:4], 0)
    fill(T.neg[:, :], -BIG)
    s_eq, s_t1, s_st, s_ga, s_sel, s_eo = vs(), vs(), vs(), vs(), vs(), vs()
    V.wait_ge(sem.io_p, 1)
    V.tensor_scalar(T.sel[:, :], T.pm[:, :], 0.0, None, A.is_equal).then_inc(s_sel, 1)

    def offsets(out, b):
        s = vs()
        if b == 0:
            V.tensor_scalar(out, T.ix[:, :], float(PAD), float(PAD + 2 * R), A.add, A.min).then_inc(s, 1)
        else:
            V.tensor_scalar(out, T.ix[:, :], float(PAD - b), float(PAD - 1), A.add, A.max).then_inc(s, 1)
        return s
    V.wait_ge(sem.ldi, 128)
    s_lo = offsets(T.lo[:, :], fbase)
    Y.wait_ge(s_lo, 1)
    load(Y, 1)

    V.wait_ge(sem.lde, 48)
    V.wait_ge(f_ep, 1)
    V.tensor_tensor(T.eq[:, :], T.en[:, :], T.ep[:, 3:19], A.is_equal).then_inc(s_eq, 1)
    V.wait_ge(sem.io_d, 1)
    V.wait_ge(s_eq, 1)
    V.tensor_tensor(T.t1[:, :], T.eq[:, :], T.dmp[:, :], A.mult).then_inc(s_t1, 1)
    V.wait_ge(s_t1, 1)
    V.tensor_tensor(T.pk[:, 0:16], T.en[:, :], T.t1[:, :], A.max).then_inc(s_st, 1)
    V.wait_ge(s_st, 1)
    V.tensor_scalar(T.pk[:, 16:32], T.pk[:, 0:16], float(DUMP), -1.0, A.min, A.add).then_inc(s_ga, 1)
    g.tensor.wait_ge(s_sel, 1)
    g.tensor.wait_ge(s_ga, 1)
    g.tensor.matmul(T.ps[:, :], T.sel[:, :], T.pk[:, :], True, True).then_inc(sem.pe, 1)
    V.wait_ge(sem.pe, 1)
    V.tensor_copy(T.eo[:, :], T.ps[:, :]).then_inc(s_eo, 1)
    s_oo = offsets(T.oo[:, :], base)
    fill(T.so[:, NL:NL + 8], 0.0)
    fill(T.sf[:, NL:NL + 8], 0.0)
    fill(T.capf[:, :], BIG)
    fill(T.capo[:, :], BIG)
    for s in fills:
        V.wait_ge(s, 1)

    def scatter(cap, off):
        s = vs()
        V.tensor_copy(cap[:, :].indirect(off[:, 0:16]), T.neg[:, :]).then_inc(s, 1)
        return s
    V.wait_ge(s_eo, 1)
    c_own = scatter(T.capo, T.eo)

    sent = 0
    g.wait_ge(s_lo, 1)
    sent += push(g, T, topo, core, out_relay, T.rl[:, 0:128], T.lo[:, 0:128], "ls0")
    sent += push(g, T, topo, core, in_relay, T.rl[:, 128:256], T.lo[:, 128:256], "ls1")
    g.wait_ge(s_eo, 1)
    sent += push(g, T, topo, core, out_relay, T.fe[:], T.eo[:], "ends")
    for a, b, need in SWAPS:
        for c in need:
            g.wait_ge(sem["tb%d" % c], 16)
        ap = T.win[:, mine + a:mine + b]
        sent += push(g, T, topo, core, mcore, ap, ap, "mate")

    nm = len(SWAPS) * bits(topo.mask(mcore, core))
    nl, no = bits(topo.mask(in_relay, core)), bits(topo.mask(out_relay, core))
    V.wait_ge(sem.ends, nl)
    c_far = scatter(T.capf, T.fe)

    for q in (V, S):
        q.wait_ge(sem.ls0, nl)
        for c in range(len(LOADS)):
            q.wait_ge(sem["tb%d" % c], 16)
        q.wait_ge(sem.mate, nm)
    for s in fills[:2]:
        S.wait_ge(s, 1)
    S.wait_ge(sem.ls1, no)
    S.wait_ge(s_oo, 1)
    nsc = [0]

    def sgather(out, off, cuts):
        done = []
        for a, b in zip(cuts[:-1], cuts[1:]):
            s = sem["sc%d" % nsc[0]]
            nsc[0] += 1
            S.activation(out[:, a:b], T.win[:, :].indirect(off[:, a // 16:b // 16]), ActivationFunctionType.Copy).then_inc(s, 1)
            done.append((s, a, b))
        return done
    part_f = sgather(T.gf, T.fl, FCUTS)
    part_o = sgather(T.go, T.oo, OCUTS)

    def states(gath, st, cap, c_done, off, parts):
        v = parts[0][1]
        s = vs()
        V.tensor_copy(gath[:, 0:v], T.win[:, :].indirect(off[:, 0:v // 16])).then_inc(s, 1)
        V.wait_ge(c_done, 1)
        prev = None
        for s_in, a, b in [(s, 0, v)] + parts:
            V.wait_ge(s_in, 1)
            if prev is not None:
                V.wait_ge(prev, 1)
            init = -BIG if prev is None else st[:, a - 1:a]
            prev = vs()
            V.tensor_tensor_scan(st[:, a:b], cap[:, a:b], gath[:, a:b], init, A.min, A.max).then_inc(prev, 1)
        V.wait_ge(prev, 1)

    states(T.gf, T.sf, T.capf, c_far, T.fl, part_f)
    s_pf = vs()
    V.tensor_copy(T.pf[:, :], T.sf[:, :].indirect(T.fe[:, 16:32])).then_inc(s_pf, 1)
    g.wait_ge(s_pf, 1)
    sent += push(g, T, topo, core, in_relay, T.pr[:, 0:HB], T.pf[:, 0:HB], "prt0")
    sent += push(g, T, topo, core, out_relay, T.pr[:, HB:NB], T.pf[:, HB:NB], "prt1")

    V.wait_ge(s_oo, 1)
    states(T.go, T.so, T.capo, c_own, T.oo, part_o)
    V.wait_ge(sem.fin, nl + no)
    s_y = vs()
    V.tensor_tensor(T.yo[:, :], T.so[:, :].indirect(T.eo[:, 16:32]), T.ph[:, :], A.max).then_inc(s_y, 1)
    Y.wait_ge(s_y, 1)
    Y.dma_start(T.y[:, :], T.yo[:, :]).then_inc(sem.sty, 16)
    Y.wait_ge(sem.sty, 16)
    g.wait_ge(sem.sent, sent)
